import numpy as np
import ml_dtypes


def mxq(x, axis, fmt="e4m3"):
    dtype, down = {"e4m3": (ml_dtypes.float8_e4m3fn, 7), "e5m2": (ml_dtypes.float8_e5m2, 14)}[fmt]
    v = np.moveaxis(np.asarray(x, np.float32).astype(ml_dtypes.bfloat16).astype(np.float64), axis, -1)
    blocks = v.reshape(v.shape[:-1] + (-1, 32))
    amax = np.abs(blocks).max(-1, keepdims=True)
    byte = np.maximum(np.where(amax > 0, np.frexp(amax)[1] - 1 + 127, 0) - down, 1)
    scale = np.exp2(byte - 127.0)
    codes = (blocks / scale).astype(np.float32).astype(dtype).astype(np.float64)
    return np.moveaxis((codes * scale).reshape(v.shape), -1, axis)


WIDE = False


def mx_kscale(k):
    if not WIDE:
        return np.ones(k)
    levels = np.array([10, -10, 5, -5, 0])
    if k % 512:
        return np.exp2(np.random.permutation(np.resize(levels, k // 32))).repeat(32)
    a = np.empty((k // 512, 16))
    for p in range(k // 512):
        a[p, :8] = np.random.permutation(np.resize(levels, 8))
        for g in range(8):
            far = levels[np.abs(levels - a[p, g]) >= 10]
            a[p, g + 8] = far[np.random.randint(len(far))]
    return np.exp2(a.ravel()).repeat(32)


BF16 = ml_dtypes.bfloat16


def bf(x):
    return np.asarray(x, np.float32).astype(BF16)


def f64(x):
    return np.asarray(x).astype(np.float64)


B, I, J, P, Q = 4, 512, 512, 512, 512


def silu(v):
    return v / (1.0 + np.exp(-v))


def two_sided(xq, a, b):
    t = xq @ mxq(f64(b), 0, "e4m3")
    return mxq(f64(a), 1, "e4m3") @ mxq(t, 1, "e4m3")


def draw0():
    s, u = mx_kscale(J), mx_kscale(I)
    x = np.random.standard_normal((B, I, J)) * s[None, None, :] * u[None, :, None]
    b1 = np.random.standard_normal((J, Q)) / np.sqrt(J) / s[:, None]
    b2 = np.random.standard_normal((J, Q)) / np.sqrt(J) / s[:, None]
    a1 = np.random.standard_normal((P, I)) / np.sqrt(I) / u[None, :]
    a2 = np.random.standard_normal((P, I)) / np.sqrt(I) / u[None, :]
    c = 0.5 * np.random.standard_normal((P, Q))
    return {"x": bf(x), "b1": bf(b1), "b2": bf(b2), "a1": bf(a1), "a2": bf(a2), "c": bf(c)}


def core(x, b1, b2, a1, a2, c):
    xq = mxq(f64(x), 2, "e4m3")
    u1 = two_sided(xq, a1, b1)
    u2 = two_sided(xq, a2, b2)
    z = u1 + u2 + f64(c)[None, :, :]
    return silu(z)


def e4m3fn_bytes(y):
    return np.clip(np.asarray(y, np.float64), -448.0, 448.0).astype(np.float32).astype(ml_dtypes.float8_e4m3fn).view(np.uint8)


def e4m3fn_values(b):
    return np.asarray(b, np.uint8).view(ml_dtypes.float8_e4m3fn).astype(np.float64)


def setup_inputs():
    d = draw0()
    x0 = np.asarray(d['b2']).astype(np.float64)
    s = (np.max(np.abs(x0), axis=(1,), keepdims=True) / 448.0).astype(np.float32)
    out = {}
    for k, v in d.items():
        if k == 'b2':
            out['b2_bytes'] = e4m3fn_bytes(x0 / s.astype(np.float64))
            out['b2_scale'] = s
        else:
            out[k] = v
    return out


def reference(x, b1, b2_bytes, b2_scale, a1, a2, c):
    return core(x, b1, e4m3fn_values(b2_bytes) * b2_scale.astype(np.float64), a1, a2, c)

@@ -1,0 +1,284 @@
+from contextlib import ExitStack
+
+import concourse.mybir as mybir
+from concourse.masks import make_identity
+
+F32 = mybir.dt.float32
+BF16 = mybir.dt.bfloat16
+U32 = mybir.dt.uint32
+U8 = mybir.dt.uint8
+FP8 = mybir.dt.float8_e4m3fn
+FP8X4 = mybir.dt.float8_e4m3fn_x4
+ACT = mybir.ActivationFunctionType
+ALU = mybir.AluOpType
+
+BATCH = 4
+DIM = 512
+P = 128
+PACK = 4
+HALF = 256
+CHUNK = 128
+WARM = 7
+
+FLOPS = BATCH * 4 * 2 * DIM * DIM * DIM
+
+
+def tile_ranktwokroneckersumlayer_kernel(tc, x, b1, b2_bytes, b2_scale, a1, a2, c, out):
+    nc = tc.nc
+
+    with ExitStack() as ctx:
+        keep = ctx.enter_context(tc.tile_pool(name="keep", bufs=1))
+        mid_sb = ctx.enter_context(tc.tile_pool(name="mid_sb", bufs=8))
+        fin = ctx.enter_context(tc.tile_pool(name="fin", bufs=6))
+        ps_turn = ctx.enter_context(tc.psum_pool(name="ps_turn", bufs=2))
+        ps_mid = ctx.enter_context(tc.psum_pool(name="ps_mid", bufs=4))
+        ps_fin = ctx.enter_context(tc.psum_pool(name="ps_fin", bufs=2))
+        ctx.enter_context(tc.manual_schedule())
+
+        ident = keep.tile([P, P], F32, name="ident")
+        warm = keep.tile([P, 1], F32, name="warm")
+        nc.vector.memset(warm[:], 0.0)
+        nc.scalar.activation(out=warm[:], in_=warm[:], func=ACT.Silu)
+        zeros = keep.tile([P, DIM], BF16, name="zeros")
+        nc.vector.memset(zeros[:], 0.0)
+        make_identity(nc, ident[:])
+        dummy = ps_fin.tile([P, DIM], F32, name="fin_bank")
+        for i in range(WARM):
+            nc.tensor.matmul(dummy[:], zeros[:, 0:P], zeros[:], start=True, stop=True)
+
+        row_slots = "(m t) k -> m t k"
+        x_raw = []
+        for n in range(BATCH):
+            raw = keep.tile([P, PACK, DIM], BF16, name=f"x_raw{n}")
+            x_raw.append(raw)
+        a_raw = [keep.tile([P, PACK, DIM], BF16, name=f"a_raw{b}") for b in range(2)]
+        b1_raw = keep.tile([P, PACK, DIM], BF16, name="b1_raw")
+        b2_codes = keep.tile([P, PACK, DIM], U8, name="b2_codes")
+        b2_rows = keep.tile([P, PACK], F32, name="b2_rows")
+        c_sb = keep.tile([P, PACK, DIM], BF16, name="c_sb")
+
+        def x_view(n):
+            return x[n, :, :].rearrange(row_slots, t=PACK)
+
+        nc.sync.dma_start(out=b1_raw[:], in_=b1.rearrange("(p j) q -> p j q", j=PACK))
+        nc.sync.dma_start(out=x_raw[0][:, 0:2, :], in_=x_view(0)[:, 0:2, :])
+        nc.sync.dma_start(out=x_raw[0][:, 2:4, :], in_=x_view(0)[:, 2:4, :])
+        nc.sync.dma_start(out=b2_rows[:], in_=b2_scale.rearrange("(p j) o -> p (j o)", j=PACK))
+        nc.sync.dma_start(out=b2_codes[:], in_=b2_bytes.rearrange("(p j) q -> p j q", j=PACK))
+        nc.sync.dma_start(out=a_raw[0][:], in_=a1.rearrange(row_slots, t=PACK))
+        nc.sync.dma_start(out=a_raw[1][:], in_=a2.rearrange(row_slots, t=PACK))
+        nc.sync.dma_start(out=x_raw[1][:], in_=x_view(1))
+        nc.sync.dma_start(out=c_sb[:], in_=c.rearrange(row_slots, t=PACK))
+        nc.sync.dma_start(out=x_raw[2][:], in_=x_view(2))
+        nc.sync.dma_start(out=x_raw[3][:], in_=x_view(3))
+
+        def copy(engine, dst, src):
+            if engine == "V":
+                nc.vector.tensor_copy(out=dst, in_=src)
+            else:
+                nc.scalar.copy(out=dst, in_=src)
+
+        def quantise(grouped, codes, scales):
+            nc.vector.quantize_mx(out=codes.bitcast(FP8X4), scales=scales, in_=grouped)
+
+        def turned_operand(nm):
+            return {
+                "grouped": keep.tile([P, DIM, PACK], BF16, name=nm + "_grouped", align_bytes=64),
+                "codes": keep.tile([P, DIM], U32, name=nm + "_codes", align_bytes=64),
+                "scales": keep.tile([P, DIM], U8, name=nm + "_scales", align_bytes=64),
+            }
+
+        def turn(raw, pair):
+            words = raw[:].rearrange("m t k -> m (t k)").bitcast(F32)
+            bank = ps_turn.tile([P, 2, 2, P], F32, name="turn_bank")
+            for s in range(2):
+                base = 256 * (2 * pair + s)
+                for u in range(2):
+                    nc.tensor.transpose(bank[:, s, u, :], words[:, base + u : base + 256 : 2], ident[:])
+            return bank
+
+        def turn_copy(engine, op, bank, pair):
+            words = op["grouped"][:].rearrange("p r j -> p (r j)").bitcast(F32)
+            dst = words[:, 512 * pair : 512 * (pair + 1)].rearrange("p (s r u) -> p s r u", s=2, u=2)
+            copy(engine, dst, bank[:].rearrange("p s u r -> p s r u"))
+
+        def turn_quantise(op, pair):
+            cols = slice(HALF * pair, HALF * (pair + 1))
+            grouped = op["grouped"][:].rearrange("p r j -> p (r j)")
+            quantise(grouped[:, 1024 * pair : 1024 * (pair + 1)], op["codes"][:, cols], op["scales"][:, cols])
+
+        xs = [turned_operand(f"x{n}") for n in range(BATCH)]
+        aa = [turned_operand(f"a{b}") for b in range(2)]
+        b_grouped = [[keep.tile([P, HALF, PACK], BF16, name=f"bg{b}{h}", align_bytes=64) for h in range(2)] for b in range(2)]
+        b_codes = [[keep.tile([P, HALF], U32, name=f"bc{b}{h}", align_bytes=64) for h in range(2)] for b in range(2)]
+        b_scales = [[keep.tile([P, HALF], U8, name=f"bs{b}{h}", align_bytes=64) for h in range(2)] for b in range(2)]
+        b2_wide = keep.tile([P, PACK, DIM], BF16, name="b2_wide")
+
+        def widen(engine, h):
+            for j in range(PACK):
+                if engine == "V":
+                    nc.vector.tensor_scalar(
+                        out=b2_wide[:, j, HALF * h : HALF * (h + 1)],
+                        in0=b2_codes[:, j, HALF * h : HALF * (h + 1)].bitcast(FP8),
+                        scalar1=b2_rows[:, j : j + 1],
+                        scalar2=None,
+                        op0=ALU.mult,
+                    )
+                    continue
+                nc.scalar.activation(
+                    out=b2_wide[:, j, HALF * h : HALF * (h + 1)],
+                    in_=b2_codes[:, j, HALF * h : HALF * (h + 1)].bitcast(FP8),
+                    func=ACT.Copy,
+                    scale=b2_rows[:, j : j + 1],
+                )
+
+        def group_b(engine, b, h):
+            src = (b1_raw, b2_wide)[b]
+            copy(engine, b_grouped[b][h][:], src[:, :, HALF * h : HALF * (h + 1)].rearrange("p j q -> p q j"))
+
+        def quantise_b(b, h):
+            quantise(b_grouped[b][h][:].rearrange("p q j -> p (q j)"), b_codes[b][h][:], b_scales[b][h][:])
+
+        units = [(n, h) for n in range(BATCH) for h in range(2)]
+        t_grouped, t_codes, t_scales, sums = {}, {}, {}, {}
+
+        def first_product(s, b, q):
+            n, h = units[s]
+            bank = ps_mid.tile([P, PACK, CHUNK], F32, name="mid_bank")
+            cols = slice(CHUNK * q, CHUNK * (q + 1))
+            for t in range(PACK):
+                rows = slice(P * t, P * (t + 1))
+                nc.tensor.matmul_mx(
+                    out=bank[:, t, :],
+                    lhsT=xs[n]["codes"][:, rows].bitcast(FP8X4),
+                    lhsT_scale=xs[n]["scales"][:, rows],
+                    rhs=b_codes[b][h][:, cols].bitcast(FP8X4),
+                    rhs_scale=b_scales[b][h][:, cols],
+                    start=True,
+                    stop=True,
+                )
+            return bank
+
+        def first_copy(engine, s, b, q, bank):
+            copy(engine, t_grouped[s][:, b, CHUNK * q : CHUNK * (q + 1), :], bank[:].rearrange("p t q -> p q t"))
+
+        def quantise_t(s):
+            t_codes[s] = mid_sb.tile([P, 2, HALF], U32, name="t_codes", align_bytes=64)
+            t_scales[s] = mid_sb.tile([P, 2, HALF], U8, name="t_scales", align_bytes=64)
+            quantise(
+                t_grouped[s][:].rearrange("p b q j -> p (b q j)"),
+                t_codes[s][:].rearrange("p b q -> p (b q)"),
+                t_scales[s][:].rearrange("p b q -> p (b q)"),
+            )
+
+        def second_product(s, pair):
+            n, h = units[s]
+            bank = ps_fin.tile([P, 2, HALF], F32, name="fin_bank")
+            for i in range(2):
+                rows = slice(P * (2 * pair + i), P * (2 * pair + i + 1))
+                for b in range(2):
+                    nc.tensor.matmul_mx(
+                        out=bank[:, i, :],
+                        lhsT=aa[b]["codes"][:, rows].bitcast(FP8X4),
+                        lhsT_scale=aa[b]["scales"][:, rows],
+                        rhs=t_codes[s][:, b, :].bitcast(FP8X4),
+                        rhs_scale=t_scales[s][:, b, :],
+                        start=(b == 0),
+                        stop=(b == 1),
+                    )
+            return bank
+
+        def add_c(s, pair, bank):
+            n, h = units[s]
+            z = fin.tile([P, 2, HALF], F32, name="z")
+            sums[(s, pair)] = z
+            nc.vector.tensor_tensor(
+                out=z[:], in0=bank[:], in1=c_sb[:, 2 * pair : 2 * pair + 2, HALF * h : HALF * (h + 1)], op=ALU.add
+            )
+
+        def finish(s, pair):
+            n, h = units[s]
+            o = fin.tile([P, 2, HALF], F32, name="o")
+            nc.scalar.activation(out=o[:], in_=sums[(s, pair)][:], func=ACT.Silu)
+            dst = out[n, :, :].rearrange("(m t) q -> m t q", t=PACK)
+            nc.sync.dma_start(out=dst[:, 2 * pair : 2 * pair + 2, HALF * h : HALF * (h + 1)], in_=o[:])
+
+        banks = {}
+
+        def turn_both(key, raw):
+            banks[key] = [turn(raw, 0), turn(raw, 1)]
+
+        def quantise_all(op):
+            quantise(op["grouped"][:].rearrange("p r j -> p (r j)"), op["codes"][:], op["scales"][:])
+
+        def first(n, k, engine):
+            s, i = 2 * n + k // 4, k % 4
+            if n < BATCH:
+                if s not in t_grouped:
+                    t_grouped[s] = mid_sb.tile([P, 2, HALF, PACK], BF16, name="t_grouped", align_bytes=64)
+                first_copy(engine, s, i // 2, i % 2, first_product(s, i // 2, i % 2))
+
+        def second(n, p):
+            if 0 <= n < BATCH:
+                s, q = 2 * n + p // 2, p % 2
+                add_c(s, q, second_product(s, q))
+
+        def last(n, p):
+            if 0 <= n < BATCH:
+                finish(2 * n + p // 2, p % 2)
+
+        turn_both("x0", x_raw[0])
+        group_b("V", 0, 1)
+        group_b("S", 0, 0)
+        quantise_b(0, 1)
+        quantise_b(0, 0)
+        turn_copy("V", xs[0], banks["x0"][0], 0)
+        turn_copy("V", xs[0], banks["x0"][1], 1)
+        widen("S", 0)
+        turn_quantise(xs[0], 1)
+        turn_quantise(xs[0], 0)
+        widen("S", 1)
+        b_a01 = turn(a_raw[0], 1)
+        turn_copy("V", aa[0], b_a01, 1)
+        b_a11 = turn(a_raw[1], 1)
+        group_b("V", 1, 0)
+        quantise_b(1, 0)
+        turn_copy("V", aa[1], b_a11, 1)
+        group_b("S", 1, 1)
+        b_a10 = turn(a_raw[1], 0)
+        turn_copy("S", aa[1], b_a10, 0)
+        quantise_b(1, 1)
+        quantise_all(aa[1])
+        for n in range(BATCH + 1):
+            first(n, 0, "V")
+            first(n, 1, "S")
+            first(n, 2, "V")
+            first(n, 3, "S")
+            if n + 1 < BATCH:
+                turn_both(f"x{n+1}", x_raw[n + 1])
+                turn_copy("V", xs[n + 1], banks[f"x{n+1}"][0], 0)
+                turn_copy("S", xs[n + 1], banks[f"x{n+1}"][1], 1)
+                quantise_all(xs[n + 1])
+            first(n, 4, "S")
+            first(n, 5, "S")
+            second(n - 1, 0)
+            first(n, 6, "S")
+            first(n, 7, "S")
+            if n < BATCH:
+                quantise_t(2 * n)
+            if n == 0:
+                b_a00 = turn(a_raw[0], 0)
+                turn_copy("S", aa[0], b_a00, 0)
+                quantise_all(aa[0])
+            second(n - 1, 1)
+            second(n - 1, 2)
+            last(n - 1, 0)
+            last(n - 1, 1)
+            last(n - 1, 2)
+            if n < BATCH:
+                quantise_t(2 * n + 1)
+            second(n - 2, 3)
+            last(n - 2, 3)
+        for n in range(BATCH + 1 - 2, BATCH):
+            second(n, 3)
+            last(n, 3)

@@ -18,7 +18,7 @@ P = 128
 PACK = 4
 HALF = 256
 CHUNK = 128
-WARM = 7
+WARM = 14
 
 FLOPS = BATCH * 4 * 2 * DIM * DIM * DIM
 
@@ -28,43 +28,48 @@ def tile_ranktwokroneckersumlayer_kernel(tc, x, b1, b2_bytes, b2_scale, a1, a2, 
 
     with ExitStack() as ctx:
         keep = ctx.enter_context(tc.tile_pool(name="keep", bufs=1))
-        mid_sb = ctx.enter_context(tc.tile_pool(name="mid_sb", bufs=8))
-        fin = ctx.enter_context(tc.tile_pool(name="fin", bufs=6))
-        ps_turn = ctx.enter_context(tc.psum_pool(name="ps_turn", bufs=2))
-        ps_mid = ctx.enter_context(tc.psum_pool(name="ps_mid", bufs=4))
-        ps_fin = ctx.enter_context(tc.psum_pool(name="ps_fin", bufs=2))
+        fin = ctx.enter_context(tc.tile_pool(name="fin", bufs=10))
+        ps = ctx.enter_context(tc.psum_pool(name="ps", bufs=8))
         ctx.enter_context(tc.manual_schedule())
 
         ident = keep.tile([P, P], F32, name="ident")
         warm = keep.tile([P, 1], F32, name="warm")
-        nc.vector.memset(warm[:], 0.0)
-        nc.scalar.activation(out=warm[:], in_=warm[:], func=ACT.Silu)
         zeros = keep.tile([P, DIM], BF16, name="zeros")
-        nc.vector.memset(zeros[:], 0.0)
-        make_identity(nc, ident[:])
-        dummy = ps_fin.tile([P, DIM], F32, name="fin_bank")
-        for i in range(WARM):
-            nc.tensor.matmul(dummy[:], zeros[:, 0:P], zeros[:], start=True, stop=True)
-
-        row_slots = "(m t) k -> m t k"
-        x_raw = []
-        for n in range(BATCH):
-            raw = keep.tile([P, PACK, DIM], BF16, name=f"x_raw{n}")
-            x_raw.append(raw)
+        x_raw = [keep.tile([P, PACK, DIM], BF16, name=f"x_raw{n}") for n in range(BATCH)]
         a_raw = [keep.tile([P, PACK, DIM], BF16, name=f"a_raw{b}") for b in range(2)]
         b1_raw = keep.tile([P, PACK, DIM], BF16, name="b1_raw")
         b2_codes = keep.tile([P, PACK, DIM], U8, name="b2_codes")
         b2_rows = keep.tile([P, PACK], F32, name="b2_rows")
+        b2_wide = keep.tile([P, PACK, DIM], BF16, name="b2_wide")
         c_sb = keep.tile([P, PACK, DIM], BF16, name="c_sb")
+
+        def operand(name):
+            return {
+                "grouped": keep.tile([P, DIM, PACK], BF16, name=name + "_grouped", align_bytes=64),
+                "codes": keep.tile([P, DIM], U32, name=name + "_codes", align_bytes=64),
+                "scales": keep.tile([P, DIM], U8, name=name + "_scales", align_bytes=64),
+            }
+
+        xs = [operand(f"x{n}") for n in range(BATCH)]
+        aa = [operand(f"a{b}") for b in range(2)]
+        bb = [operand(f"b{b}") for b in range(2)]
+        ts = [[operand(f"t{n}{b}") for b in range(2)] for n in range(BATCH)]
+
+        nc.vector.memset(warm[:], 0.0)
+        nc.vector.memset(zeros[:], 0.0)
+        make_identity(nc, ident[:])
+
+        row_slots = "(m t) k -> m t k"
+        k_rows = "(p j) q -> p j q"
 
         def x_view(n):
             return x[n, :, :].rearrange(row_slots, t=PACK)
 
-        nc.sync.dma_start(out=b1_raw[:], in_=b1.rearrange("(p j) q -> p j q", j=PACK))
+        nc.scalar.dma_start(out=b2_rows[:], in_=b2_scale.rearrange("(p j) o -> p (j o)", j=PACK))
+        nc.sync.dma_start(out=b2_codes[:], in_=b2_bytes.rearrange(k_rows, j=PACK))
+        nc.sync.dma_start(out=b1_raw[:], in_=b1.rearrange(k_rows, j=PACK))
         nc.sync.dma_start(out=x_raw[0][:, 0:2, :], in_=x_view(0)[:, 0:2, :])
         nc.sync.dma_start(out=x_raw[0][:, 2:4, :], in_=x_view(0)[:, 2:4, :])
-        nc.sync.dma_start(out=b2_rows[:], in_=b2_scale.rearrange("(p j) o -> p (j o)", j=PACK))
-        nc.sync.dma_start(out=b2_codes[:], in_=b2_bytes.rearrange("(p j) q -> p j q", j=PACK))
         nc.sync.dma_start(out=a_raw[0][:], in_=a1.rearrange(row_slots, t=PACK))
         nc.sync.dma_start(out=a_raw[1][:], in_=a2.rearrange(row_slots, t=PACK))
         nc.sync.dma_start(out=x_raw[1][:], in_=x_view(1))
@@ -72,213 +77,256 @@ def tile_ranktwokroneckersumlayer_kernel(tc, x, b1, b2_bytes, b2_scale, a1, a2, 
         nc.sync.dma_start(out=x_raw[2][:], in_=x_view(2))
         nc.sync.dma_start(out=x_raw[3][:], in_=x_view(3))
 
+        nc.scalar.activation(out=warm[:], in_=warm[:], func=ACT.Silu)
+        dummy = ps.tile([P, DIM], F32, name="bank")
+        for i in range(WARM):
+            nc.tensor.matmul(dummy[:], zeros[:, 0:P], zeros[:], start=True, stop=True)
+
         def copy(engine, dst, src):
             if engine == "V":
                 nc.vector.tensor_copy(out=dst, in_=src)
             else:
                 nc.scalar.copy(out=dst, in_=src)
 
-        def quantise(grouped, codes, scales):
-            nc.vector.quantize_mx(out=codes.bitcast(FP8X4), scales=scales, in_=grouped)
+        def quantise(op, first=0, width=DIM):
+            cols = slice(first, first + width)
+            nc.vector.quantize_mx(
+                out=op["codes"][:, cols].bitcast(FP8X4),
+                scales=op["scales"][:, cols],
+                in_=op["grouped"][:, cols, :].rearrange("p r j -> p (r j)"),
+            )
 
-        def turned_operand(nm):
-            return {
-                "grouped": keep.tile([P, DIM, PACK], BF16, name=nm + "_grouped", align_bytes=64),
-                "codes": keep.tile([P, DIM], U32, name=nm + "_codes", align_bytes=64),
-                "scales": keep.tile([P, DIM], U8, name=nm + "_scales", align_bytes=64),
-            }
+        banks = {}
 
-        def turn(raw, pair):
+        def turn(key, raw, pair):
             words = raw[:].rearrange("m t k -> m (t k)").bitcast(F32)
-            bank = ps_turn.tile([P, 2, 2, P], F32, name="turn_bank")
+            bank = ps.tile([P, 2, 2, P], F32, name="bank")
             for s in range(2):
                 base = 256 * (2 * pair + s)
                 for u in range(2):
                     nc.tensor.transpose(bank[:, s, u, :], words[:, base + u : base + 256 : 2], ident[:])
-            return bank
+            banks[(key, pair)] = bank
 
-        def turn_copy(engine, op, bank, pair):
+        def turn_copy(engine, key, op, pair):
+            bank = banks[(key, pair)]
             words = op["grouped"][:].rearrange("p r j -> p (r j)").bitcast(F32)
             dst = words[:, 512 * pair : 512 * (pair + 1)].rearrange("p (s r u) -> p s r u", s=2, u=2)
             copy(engine, dst, bank[:].rearrange("p s u r -> p s r u"))
 
-        def turn_quantise(op, pair):
-            cols = slice(HALF * pair, HALF * (pair + 1))
-            grouped = op["grouped"][:].rearrange("p r j -> p (r j)")
-            quantise(grouped[:, 1024 * pair : 1024 * (pair + 1)], op["codes"][:, cols], op["scales"][:, cols])
-
-        xs = [turned_operand(f"x{n}") for n in range(BATCH)]
-        aa = [turned_operand(f"a{b}") for b in range(2)]
-        b_grouped = [[keep.tile([P, HALF, PACK], BF16, name=f"bg{b}{h}", align_bytes=64) for h in range(2)] for b in range(2)]
-        b_codes = [[keep.tile([P, HALF], U32, name=f"bc{b}{h}", align_bytes=64) for h in range(2)] for b in range(2)]
-        b_scales = [[keep.tile([P, HALF], U8, name=f"bs{b}{h}", align_bytes=64) for h in range(2)] for b in range(2)]
-        b2_wide = keep.tile([P, PACK, DIM], BF16, name="b2_wide")
-
-        def widen(engine, h):
-            for j in range(PACK):
-                if engine == "V":
-                    nc.vector.tensor_scalar(
-                        out=b2_wide[:, j, HALF * h : HALF * (h + 1)],
-                        in0=b2_codes[:, j, HALF * h : HALF * (h + 1)].bitcast(FP8),
-                        scalar1=b2_rows[:, j : j + 1],
-                        scalar2=None,
-                        op0=ALU.mult,
-                    )
-                    continue
-                nc.scalar.activation(
-                    out=b2_wide[:, j, HALF * h : HALF * (h + 1)],
-                    in_=b2_codes[:, j, HALF * h : HALF * (h + 1)].bitcast(FP8),
-                    func=ACT.Copy,
-                    scale=b2_rows[:, j : j + 1],
+        def widen(engine, j):
+            src = b2_codes[:, j, :].bitcast(FP8)
+            if engine == "V":
+                nc.vector.tensor_scalar(
+                    out=b2_wide[:, j, :], in0=src, scalar1=b2_rows[:, j : j + 1], scalar2=None, op0=ALU.mult
                 )
+            else:
+                nc.scalar.activation(out=b2_wide[:, j, :], in_=src, func=ACT.Copy, scale=b2_rows[:, j : j + 1])
 
         def group_b(engine, b, h):
             src = (b1_raw, b2_wide)[b]
-            copy(engine, b_grouped[b][h][:], src[:, :, HALF * h : HALF * (h + 1)].rearrange("p j q -> p q j"))
+            cols = slice(HALF * h, HALF * (h + 1))
+            copy(engine, bb[b]["grouped"][:, cols, :], src[:, :, cols].rearrange("p j q -> p q j"))
 
         def quantise_b(b, h):
-            quantise(b_grouped[b][h][:].rearrange("p q j -> p (q j)"), b_codes[b][h][:], b_scales[b][h][:])
+            quantise(bb[b], HALF * h, HALF)
 
-        units = [(n, h) for n in range(BATCH) for h in range(2)]
-        t_grouped, t_codes, t_scales, sums = {}, {}, {}, {}
+        def mx(bank, left, rows, right, cols, start, stop):
+            nc.tensor.matmul_mx(
+                out=bank,
+                lhsT=left["codes"][:, rows].bitcast(FP8X4),
+                lhsT_scale=left["scales"][:, rows],
+                rhs=right["codes"][:, cols].bitcast(FP8X4),
+                rhs_scale=right["scales"][:, cols],
+                start=start,
+                stop=stop,
+            )
 
-        def first_product(s, b, q):
-            n, h = units[s]
-            bank = ps_mid.tile([P, PACK, CHUNK], F32, name="mid_bank")
-            cols = slice(CHUNK * q, CHUNK * (q + 1))
+        def first(n, b, q):
+            bank = ps.tile([P, PACK, CHUNK], F32, name="bank")
             for t in range(PACK):
-                rows = slice(P * t, P * (t + 1))
-                nc.tensor.matmul_mx(
-                    out=bank[:, t, :],
-                    lhsT=xs[n]["codes"][:, rows].bitcast(FP8X4),
-                    lhsT_scale=xs[n]["scales"][:, rows],
-                    rhs=b_codes[b][h][:, cols].bitcast(FP8X4),
-                    rhs_scale=b_scales[b][h][:, cols],
-                    start=True,
-                    stop=True,
-                )
-            return bank
+                mx(bank[:, t, :], xs[n], slice(P * t, P * (t + 1)), bb[b], slice(CHUNK * q, CHUNK * (q + 1)), True, True)
+            banks[(n, b, q)] = bank
 
-        def first_copy(engine, s, b, q, bank):
-            copy(engine, t_grouped[s][:, b, CHUNK * q : CHUNK * (q + 1), :], bank[:].rearrange("p t q -> p q t"))
+        def first_copy(engine, n, b, q):
+            dst = ts[n][b]["grouped"][:, CHUNK * q : CHUNK * (q + 1), :]
+            copy(engine, dst, banks[(n, b, q)][:].rearrange("p t q -> p q t"))
 
-        def quantise_t(s):
-            t_codes[s] = mid_sb.tile([P, 2, HALF], U32, name="t_codes", align_bytes=64)
-            t_scales[s] = mid_sb.tile([P, 2, HALF], U8, name="t_scales", align_bytes=64)
-            quantise(
-                t_grouped[s][:].rearrange("p b q j -> p (b q j)"),
-                t_codes[s][:].rearrange("p b q -> p (b q)"),
-                t_scales[s][:].rearrange("p b q -> p (b q)"),
-            )
+        def second(n, t):
+            bank = ps.tile([P, DIM], F32, name="bank")
+            for b in range(2):
+                mx(bank[:], aa[b], slice(P * t, P * (t + 1)), ts[n][b], slice(0, DIM), b == 0, b == 1)
+            banks[("z", n, t)] = bank
 
-        def second_product(s, pair):
-            n, h = units[s]
-            bank = ps_fin.tile([P, 2, HALF], F32, name="fin_bank")
-            for i in range(2):
-                rows = slice(P * (2 * pair + i), P * (2 * pair + i + 1))
-                for b in range(2):
-                    nc.tensor.matmul_mx(
-                        out=bank[:, i, :],
-                        lhsT=aa[b]["codes"][:, rows].bitcast(FP8X4),
-                        lhsT_scale=aa[b]["scales"][:, rows],
-                        rhs=t_codes[s][:, b, :].bitcast(FP8X4),
-                        rhs_scale=t_scales[s][:, b, :],
-                        start=(b == 0),
-                        stop=(b == 1),
-                    )
-            return bank
+        def add_c(n, t):
+            z = fin.tile([P, DIM], F32, name="z")
+            nc.vector.tensor_tensor(out=z[:], in0=banks[("z", n, t)][:], in1=c_sb[:, t, :], op=ALU.add)
+            banks[("s", n, t)] = z
 
-        def add_c(s, pair, bank):
-            n, h = units[s]
-            z = fin.tile([P, 2, HALF], F32, name="z")
-            sums[(s, pair)] = z
-            nc.vector.tensor_tensor(
-                out=z[:], in0=bank[:], in1=c_sb[:, 2 * pair : 2 * pair + 2, HALF * h : HALF * (h + 1)], op=ALU.add
-            )
+        def finish(n, t):
+            o = fin.tile([P, DIM], F32, name="o")
+            nc.scalar.activation(out=o[:], in_=banks[("s", n, t)][:], func=ACT.Silu)
+            nc.sync.dma_start(out=out[n, :, :].rearrange("(m t) q -> m t q", t=PACK)[:, t, :], in_=o[:])
 
-        def finish(s, pair):
-            n, h = units[s]
-            o = fin.tile([P, 2, HALF], F32, name="o")
-            nc.scalar.activation(out=o[:], in_=sums[(s, pair)][:], func=ACT.Silu)
-            dst = out[n, :, :].rearrange("(m t) q -> m t q", t=PACK)
-            nc.sync.dma_start(out=dst[:, 2 * pair : 2 * pair + 2, HALF * h : HALF * (h + 1)], in_=o[:])
-
-        banks = {}
-
-        def turn_both(key, raw):
-            banks[key] = [turn(raw, 0), turn(raw, 1)]
-
-        def quantise_all(op):
-            quantise(op["grouped"][:].rearrange("p r j -> p (r j)"), op["codes"][:], op["scales"][:])
-
-        def first(n, k, engine):
-            s, i = 2 * n + k // 4, k % 4
-            if n < BATCH:
-                if s not in t_grouped:
-                    t_grouped[s] = mid_sb.tile([P, 2, HALF, PACK], BF16, name="t_grouped", align_bytes=64)
-                first_copy(engine, s, i // 2, i % 2, first_product(s, i // 2, i % 2))
-
-        def second(n, p):
-            if 0 <= n < BATCH:
-                s, q = 2 * n + p // 2, p % 2
-                add_c(s, q, second_product(s, q))
-
-        def last(n, p):
-            if 0 <= n < BATCH:
-                finish(2 * n + p // 2, p % 2)
-
-        turn_both("x0", x_raw[0])
+        widen("V", 3)
+        widen("S", 2)
+        widen("V", 1)
+        turn("x0", x_raw[0], 1)
         group_b("V", 0, 1)
-        group_b("S", 0, 0)
         quantise_b(0, 1)
-        quantise_b(0, 0)
-        turn_copy("V", xs[0], banks["x0"][0], 0)
-        turn_copy("V", xs[0], banks["x0"][1], 1)
+        turn_copy("V", "x0", xs[0], 1)
         widen("S", 0)
-        turn_quantise(xs[0], 1)
-        turn_quantise(xs[0], 0)
-        widen("S", 1)
-        b_a01 = turn(a_raw[0], 1)
-        turn_copy("V", aa[0], b_a01, 1)
-        b_a11 = turn(a_raw[1], 1)
         group_b("V", 1, 0)
-        quantise_b(1, 0)
-        turn_copy("V", aa[1], b_a11, 1)
+        turn("x0", x_raw[0], 0)
+        group_b("S", 0, 0)
         group_b("S", 1, 1)
-        b_a10 = turn(a_raw[1], 0)
-        turn_copy("S", aa[1], b_a10, 0)
         quantise_b(1, 1)
-        quantise_all(aa[1])
-        for n in range(BATCH + 1):
-            first(n, 0, "V")
-            first(n, 1, "S")
-            first(n, 2, "V")
-            first(n, 3, "S")
-            if n + 1 < BATCH:
-                turn_both(f"x{n+1}", x_raw[n + 1])
-                turn_copy("V", xs[n + 1], banks[f"x{n+1}"][0], 0)
-                turn_copy("S", xs[n + 1], banks[f"x{n+1}"][1], 1)
-                quantise_all(xs[n + 1])
-            first(n, 4, "S")
-            first(n, 5, "S")
-            second(n - 1, 0)
-            first(n, 6, "S")
-            first(n, 7, "S")
-            if n < BATCH:
-                quantise_t(2 * n)
-            if n == 0:
-                b_a00 = turn(a_raw[0], 0)
-                turn_copy("S", aa[0], b_a00, 0)
-                quantise_all(aa[0])
-            second(n - 1, 1)
-            second(n - 1, 2)
-            last(n - 1, 0)
-            last(n - 1, 1)
-            last(n - 1, 2)
-            if n < BATCH:
-                quantise_t(2 * n + 1)
-            second(n - 2, 3)
-            last(n - 2, 3)
-        for n in range(BATCH + 1 - 2, BATCH):
-            second(n, 3)
-            last(n, 3)
+        quantise_b(1, 0)
+        quantise_b(0, 0)
+        turn("a0", a_raw[0], 0)
+        turn_copy("S", "x0", xs[0], 0)
+        quantise(xs[0], 0, HALF)
+        turn("a0", a_raw[0], 1)
+        turn_copy("S", "a0", aa[0], 0)
+        turn_copy("S", "a0", aa[0], 1)
+        turn("a1", a_raw[1], 1)
+        quantise(xs[0], 256, HALF)
+        turn_copy("S", "a1", aa[1], 1)
+        quantise(aa[0])
+        turn("a1", a_raw[1], 0)
+        turn_copy("S", "a1", aa[1], 0)
+        quantise(aa[1])
+        turn("x1", x_raw[1], 0)
+        turn_copy("V", "x1", xs[1], 0)
+        turn("x1", x_raw[1], 1)
+        turn_copy("S", "x1", xs[1], 1)
+        first(0, 0, 0)
+        first_copy("V", 0, 0, 0)
+        first(0, 0, 1)
+        first_copy("S", 0, 0, 1)
+        first(0, 0, 2)
+        first_copy("S", 0, 0, 2)
+        first(0, 0, 3)
+        first_copy("S", 0, 0, 3)
+        first(0, 1, 0)
+        first_copy("S", 0, 1, 0)
+        first(0, 1, 1)
+        first_copy("S", 0, 1, 1)
+        quantise(xs[1])
+        first(0, 1, 2)
+        first_copy("S", 0, 1, 2)
+        first(0, 1, 3)
+        first_copy("V", 0, 1, 3)
+        quantise(ts[0][0])
+        turn("x2", x_raw[2], 0)
+        turn_copy("V", "x2", xs[2], 0)
+        turn("x2", x_raw[2], 1)
+        turn_copy("S", "x2", xs[2], 1)
+        first(1, 0, 0)
+        first_copy("S", 1, 0, 0)
+        quantise(ts[0][1])
+        first(1, 0, 1)
+        first_copy("S", 1, 0, 1)
+        first(1, 0, 2)
+        first_copy("V", 1, 0, 2)
+        first(1, 0, 3)
+        first_copy("S", 1, 0, 3)
+        first(1, 1, 0)
+        first_copy("V", 1, 1, 0)
+        first(1, 1, 1)
+        first_copy("S", 1, 1, 1)
+        quantise(xs[2])
+        first(1, 1, 2)
+        first_copy("S", 1, 1, 2)
+        first(1, 1, 3)
+        first_copy("V", 1, 1, 3)
+        quantise(ts[1][0])
+        turn("x3", x_raw[3], 0)
+        turn_copy("V", "x3", xs[3], 0)
+        turn("x3", x_raw[3], 1)
+        turn_copy("S", "x3", xs[3], 1)
+        first(2, 0, 0)
+        first_copy("S", 2, 0, 0)
+        quantise(ts[1][1])
+        first(2, 0, 1)
+        first_copy("V", 2, 0, 1)
+        first(2, 0, 2)
+        first_copy("S", 2, 0, 2)
+        first(2, 0, 3)
+        first_copy("S", 2, 0, 3)
+        first(2, 1, 0)
+        first_copy("S", 2, 1, 0)
+        first(2, 1, 1)
+        first_copy("V", 2, 1, 1)
+        quantise(xs[3])
+        first(2, 1, 2)
+        first_copy("S", 2, 1, 2)
+        second(0, 0)
+        first(2, 1, 3)
+        first_copy("S", 2, 1, 3)
+        second(0, 1)
+        add_c(0, 0)
+        finish(0, 0)
+        quantise(ts[2][0])
+        add_c(0, 1)
+        first(3, 0, 0)
+        first_copy("V", 3, 0, 0)
+        quantise(ts[2][1])
+        first(3, 0, 1)
+        first_copy("S", 3, 0, 1)
+        first(3, 0, 2)
+        first_copy("S", 3, 0, 2)
+        first(3, 0, 3)
+        first_copy("S", 3, 0, 3)
+        first(3, 1, 0)
+        first_copy("S", 3, 1, 0)
+        first(3, 1, 1)
+        first_copy("V", 3, 1, 1)
+        first(3, 1, 2)
+        first_copy("S", 3, 1, 2)
+        second(1, 0)
+        first(3, 1, 3)
+        first_copy("S", 3, 1, 3)
+        second(1, 1)
+        finish(0, 1)
+        add_c(1, 0)
+        finish(1, 0)
+        quantise(ts[3][0])
+        add_c(1, 1)
+        quantise(ts[3][1])
+        second(2, 0)
+        second(2, 1)
+        finish(1, 1)
+        add_c(2, 0)
+        finish(2, 0)
+        add_c(2, 1)
+        second(3, 0)
+        second(3, 1)
+        finish(2, 1)
+        add_c(3, 0)
+        finish(3, 0)
+        add_c(3, 1)
+        finish(3, 1)
+        second(0, 2)
+        add_c(0, 2)
+        second(1, 2)
+        add_c(1, 2)
+        finish(0, 2)
+        second(2, 2)
+        add_c(2, 2)
+        finish(1, 2)
+        second(3, 2)
+        add_c(3, 2)
+        finish(2, 2)
+        finish(3, 2)
+        second(0, 3)
+        second(1, 3)
+        second(2, 3)
+        second(3, 3)
+        add_c(0, 3)
+        finish(0, 3)
+        add_c(1, 3)
+        finish(1, 3)
+        add_c(2, 3)
+        finish(2, 3)
+        add_c(3, 3)
+        finish(3, 3)

@@ -19,6 +19,10 @@ PACK = 4
 HALF = 256
 CHUNK = 128
 WARM = 14
+ON_VECTOR = [[0, 7], [2, 4, 7], [1, 5], [2, 5]]
+N0POS, QPOS = 7, 2
+FINISH_EARLY = [[], [], [(0, 0)], [], [(0, 1), (1, 0), (1, 1)]]
+HEAD = [["W3", "V"], ["W2", "S"], ["W1", "V"], ["I01", "V"], ["B01", "V"], ["W0", "S"], ["I10", "V"], ["T:x00", "T"], ["T:x01", "T"], ["I00", "S"], ["I11", "S"], ["B11", "V"], ["D0", "T"], ["C:x01", "V"], ["B10", "V"], ["B00", "V"], ["T:a00", "T"], ["C:x00", "S"], ["T:a01", "T"], ["C:a00", "V"], ["C:a01", "S"], ["T:a11", "T"], ["Q:x00", "V"], ["Q:x01", "V"], ["C:a11", "S"], ["Q:a0", "V"], ["T:a10", "T"], ["C:a10", "S"], ["Q:a1", "V"], ["T1.0", "T"], ["C1.0", "V"], ["T1.1", "T"], ["C1.1", "S"]]
 
 FLOPS = BATCH * 4 * 2 * DIM * DIM * DIM
 
@@ -28,7 +32,7 @@ def tile_ranktwokroneckersumlayer_kernel(tc, x, b1, b2_bytes, b2_scale, a1, a2, 
 
     with ExitStack() as ctx:
         keep = ctx.enter_context(tc.tile_pool(name="keep", bufs=1))
-        fin = ctx.enter_context(tc.tile_pool(name="fin", bufs=10))
+        fin = ctx.enter_context(tc.tile_pool(name="fin", bufs=16))
         ps = ctx.enter_context(tc.psum_pool(name="ps", bufs=8))
         ctx.enter_context(tc.manual_schedule())
 
@@ -78,13 +82,18 @@ def tile_ranktwokroneckersumlayer_kernel(tc, x, b1, b2_bytes, b2_scale, a1, a2, 
         nc.sync.dma_start(out=x_raw[3][:], in_=x_view(3))
 
         nc.scalar.activation(out=warm[:], in_=warm[:], func=ACT.Silu)
-        dummy = ps.tile([P, DIM], F32, name="bank")
-        for i in range(WARM):
-            nc.tensor.matmul(dummy[:], zeros[:, 0:P], zeros[:], start=True, stop=True)
+        def dummies(count):
+            dummy = ps.tile([P, DIM], F32, name="bank")
+            for i in range(count):
+                nc.tensor.matmul(dummy[:], zeros[:, 0:P], zeros[:], start=True, stop=True)
+
+        dummies(WARM)
 
         def copy(engine, dst, src):
             if engine == "V":
                 nc.vector.tensor_copy(out=dst, in_=src)
+            elif engine == "G":
+                nc.gpsimd.tensor_scalar(out=dst, in0=src, scalar1=1.0, scalar2=0.0, op0=ALU.mult, op1=ALU.add)
             else:
                 nc.scalar.copy(out=dst, in_=src)
 
@@ -167,166 +176,58 @@ def tile_ranktwokroneckersumlayer_kernel(tc, x, b1, b2_bytes, b2_scale, a1, a2, 
             nc.scalar.activation(out=o[:], in_=banks[("s", n, t)][:], func=ACT.Silu)
             nc.sync.dma_start(out=out[n, :, :].rearrange("(m t) q -> m t q", t=PACK)[:, t, :], in_=o[:])
 
-        widen("V", 3)
-        widen("S", 2)
-        widen("V", 1)
-        turn("x0", x_raw[0], 1)
-        group_b("V", 0, 1)
-        quantise_b(0, 1)
-        turn_copy("V", "x0", xs[0], 1)
-        widen("S", 0)
-        group_b("V", 1, 0)
-        turn("x0", x_raw[0], 0)
-        group_b("S", 0, 0)
-        group_b("S", 1, 1)
-        quantise_b(1, 1)
-        quantise_b(1, 0)
-        quantise_b(0, 0)
-        turn("a0", a_raw[0], 0)
-        turn_copy("S", "x0", xs[0], 0)
-        quantise(xs[0], 0, HALF)
-        turn("a0", a_raw[0], 1)
-        turn_copy("S", "a0", aa[0], 0)
-        turn_copy("S", "a0", aa[0], 1)
-        turn("a1", a_raw[1], 1)
-        quantise(xs[0], 256, HALF)
-        turn_copy("S", "a1", aa[1], 1)
-        quantise(aa[0])
-        turn("a1", a_raw[1], 0)
-        turn_copy("S", "a1", aa[1], 0)
-        quantise(aa[1])
-        turn("x1", x_raw[1], 0)
-        turn_copy("V", "x1", xs[1], 0)
-        turn("x1", x_raw[1], 1)
-        turn_copy("S", "x1", xs[1], 1)
-        first(0, 0, 0)
-        first_copy("V", 0, 0, 0)
-        first(0, 0, 1)
-        first_copy("S", 0, 0, 1)
-        first(0, 0, 2)
-        first_copy("S", 0, 0, 2)
-        first(0, 0, 3)
-        first_copy("S", 0, 0, 3)
-        first(0, 1, 0)
-        first_copy("S", 0, 1, 0)
-        first(0, 1, 1)
-        first_copy("S", 0, 1, 1)
-        quantise(xs[1])
-        first(0, 1, 2)
-        first_copy("S", 0, 1, 2)
-        first(0, 1, 3)
-        first_copy("V", 0, 1, 3)
-        quantise(ts[0][0])
-        turn("x2", x_raw[2], 0)
-        turn_copy("V", "x2", xs[2], 0)
-        turn("x2", x_raw[2], 1)
-        turn_copy("S", "x2", xs[2], 1)
-        first(1, 0, 0)
-        first_copy("S", 1, 0, 0)
-        quantise(ts[0][1])
-        first(1, 0, 1)
-        first_copy("S", 1, 0, 1)
-        first(1, 0, 2)
-        first_copy("V", 1, 0, 2)
-        first(1, 0, 3)
-        first_copy("S", 1, 0, 3)
-        first(1, 1, 0)
-        first_copy("V", 1, 1, 0)
-        first(1, 1, 1)
-        first_copy("S", 1, 1, 1)
-        quantise(xs[2])
-        first(1, 1, 2)
-        first_copy("S", 1, 1, 2)
-        first(1, 1, 3)
-        first_copy("V", 1, 1, 3)
-        quantise(ts[1][0])
-        turn("x3", x_raw[3], 0)
-        turn_copy("V", "x3", xs[3], 0)
-        turn("x3", x_raw[3], 1)
-        turn_copy("S", "x3", xs[3], 1)
-        first(2, 0, 0)
-        first_copy("S", 2, 0, 0)
-        quantise(ts[1][1])
-        first(2, 0, 1)
-        first_copy("V", 2, 0, 1)
-        first(2, 0, 2)
-        first_copy("S", 2, 0, 2)
-        first(2, 0, 3)
-        first_copy("S", 2, 0, 3)
-        first(2, 1, 0)
-        first_copy("S", 2, 1, 0)
-        first(2, 1, 1)
-        first_copy("V", 2, 1, 1)
-        quantise(xs[3])
-        first(2, 1, 2)
-        first_copy("S", 2, 1, 2)
-        second(0, 0)
-        first(2, 1, 3)
-        first_copy("S", 2, 1, 3)
-        second(0, 1)
-        add_c(0, 0)
-        finish(0, 0)
-        quantise(ts[2][0])
-        add_c(0, 1)
-        first(3, 0, 0)
-        first_copy("V", 3, 0, 0)
-        quantise(ts[2][1])
-        first(3, 0, 1)
-        first_copy("S", 3, 0, 1)
-        first(3, 0, 2)
-        first_copy("S", 3, 0, 2)
-        first(3, 0, 3)
-        first_copy("S", 3, 0, 3)
-        first(3, 1, 0)
-        first_copy("S", 3, 1, 0)
-        first(3, 1, 1)
-        first_copy("V", 3, 1, 1)
-        first(3, 1, 2)
-        first_copy("S", 3, 1, 2)
-        second(1, 0)
-        first(3, 1, 3)
-        first_copy("S", 3, 1, 3)
-        second(1, 1)
-        finish(0, 1)
-        add_c(1, 0)
-        finish(1, 0)
-        quantise(ts[3][0])
-        add_c(1, 1)
-        quantise(ts[3][1])
-        second(2, 0)
-        second(2, 1)
-        finish(1, 1)
-        add_c(2, 0)
-        finish(2, 0)
-        add_c(2, 1)
-        second(3, 0)
-        second(3, 1)
-        finish(2, 1)
-        add_c(3, 0)
-        finish(3, 0)
-        add_c(3, 1)
-        finish(3, 1)
-        second(0, 2)
-        add_c(0, 2)
-        second(1, 2)
-        add_c(1, 2)
-        finish(0, 2)
-        second(2, 2)
-        add_c(2, 2)
-        finish(1, 2)
-        second(3, 2)
-        add_c(3, 2)
-        finish(2, 2)
-        finish(3, 2)
-        second(0, 3)
-        second(1, 3)
-        second(2, 3)
-        second(3, 3)
-        add_c(0, 3)
-        finish(0, 3)
-        add_c(1, 3)
-        finish(1, 3)
-        add_c(2, 3)
-        finish(2, 3)
-        add_c(3, 3)
-        finish(3, 3)
+        head_actions = {}
+        for pair in range(2):
+            head_actions[f"T:x0{pair}"] = lambda e, p=pair: turn("x0", x_raw[0], p)
+            head_actions[f"C:x0{pair}"] = lambda e, p=pair: turn_copy(e, "x0", xs[0], p)
+            head_actions[f"Q:x0{pair}"] = lambda e, p=pair: quantise(xs[0], HALF * p, HALF)
+            for b in range(2):
+                head_actions[f"T:a{b}{pair}"] = lambda e, b=b, p=pair: turn(f"a{b}", a_raw[b], p)
+                head_actions[f"C:a{b}{pair}"] = lambda e, b=b, p=pair: turn_copy(e, f"a{b}", aa[b], p)
+                head_actions[f"I{b}{pair}"] = lambda e, b=b, p=pair: group_b(e, b, p)
+                head_actions[f"B{b}{pair}"] = lambda e, b=b, p=pair: quantise_b(b, p)
+        for pair in range(2):
+            head_actions[f"T1.{pair}"] = lambda e, p=pair: turn("x1", x_raw[1], p)
+            head_actions[f"C1.{pair}"] = lambda e, p=pair: turn_copy(e, "x1", xs[1], p)
+        for b in range(2):
+            head_actions[f"Q:a{b}"] = lambda e, b=b: quantise(aa[b])
+        for j in range(PACK):
+            head_actions[f"W{j}"] = lambda e, j=j: widen(e, j)
+            head_actions[f"D{j}"] = lambda e, j=j: dummies(2)
+
+        for key, engine in HEAD:
+            head_actions[key](engine)
+
+        def whole_second(n, t):
+            second(n, t)
+            add_c(n, t)
+
+        for n in range(BATCH):
+            for k in range(8):
+                b, q = k // 4, k % 4
+                if n >= 2 and k == N0POS:
+                    second(n - 2, 0)
+                first(n, b, q)
+                first_copy("V" if k in ON_VECTOR[n] else "S", n, b, q)
+                if n + 1 < BATCH and k == QPOS:
+                    quantise(xs[n + 1])
+            if n >= 2:
+                second(n - 2, 1)
+                add_c(n - 2, 0)
+            quantise(ts[n][0])
+            if n + 2 < BATCH:
+                turn(f"x{n + 2}", x_raw[n + 2], 0)
+                turn(f"x{n + 2}", x_raw[n + 2], 1)
+                turn_copy("V", f"x{n + 2}", xs[n + 2], 0)
+                turn_copy("S", f"x{n + 2}", xs[n + 2], 1)
+            if n >= 2:
+                add_c(n - 2, 1)
+            quantise(ts[n][1])
+            for job in FINISH_EARLY[n]:
+                finish(*job)
+        tail = [(n, t) for n in range(BATCH) for t in range(PACK) if n >= 2 or t >= 2]
+        for job in FINISH_EARLY[4]:
+            finish(*job)
+        for n, t in tail:
+            whole_second(n, t)
+            finish(n, t)

from contextlib import ExitStack

import concourse.mybir as mybir
from concourse.masks import make_identity

F32 = mybir.dt.float32
BF16 = mybir.dt.bfloat16
U32 = mybir.dt.uint32
U8 = mybir.dt.uint8
FP8 = mybir.dt.float8_e4m3fn
FP8X4 = mybir.dt.float8_e4m3fn_x4
ACT = mybir.ActivationFunctionType
ALU = mybir.AluOpType

BATCH = 4
DIM = 512
P = 128
PACK = 4
HALF = 256
CHUNK = 128
WARM = 14
ON_VECTOR = [[0, 7], [2, 4, 7], [1, 5], [2, 5]]
N0POS, QPOS = 7, 2
FINISH_EARLY = [[], [], [(0, 0)], [], [(0, 1), (1, 0), (1, 1)]]
HEAD = [["W3", "V"], ["W2", "S"], ["W1", "V"], ["I01", "V"], ["B01", "V"], ["W0", "S"], ["I10", "V"], ["T:x00", "T"], ["T:x01", "T"], ["I00", "S"], ["I11", "S"], ["B11", "V"], ["D0", "T"], ["C:x01", "V"], ["B10", "V"], ["B00", "V"], ["T:a00", "T"], ["C:x00", "S"], ["T:a01", "T"], ["C:a00", "V"], ["C:a01", "S"], ["T:a11", "T"], ["Q:x00", "V"], ["Q:x01", "V"], ["C:a11", "S"], ["Q:a0", "V"], ["T:a10", "T"], ["C:a10", "S"], ["Q:a1", "V"], ["T1.0", "T"], ["C1.0", "V"], ["T1.1", "T"], ["C1.1", "S"]]

FLOPS = BATCH * 4 * 2 * DIM * DIM * DIM


def tile_ranktwokroneckersumlayer_kernel(tc, x, b1, b2_bytes, b2_scale, a1, a2, c, out):
    nc = tc.nc

    with ExitStack() as ctx:
        keep = ctx.enter_context(tc.tile_pool(name="keep", bufs=1))
        fin = ctx.enter_context(tc.tile_pool(name="fin", bufs=16))
        ps = ctx.enter_context(tc.psum_pool(name="ps", bufs=8))
        ctx.enter_context(tc.manual_schedule())

        ident = keep.tile([P, P], F32, name="ident")
        warm = keep.tile([P, 1], F32, name="warm")
        zeros = keep.tile([P, DIM], BF16, name="zeros")
        x_raw = [keep.tile([P, PACK, DIM], BF16, name=f"x_raw{n}") for n in range(BATCH)]
        a_raw = [keep.tile([P, PACK, DIM], BF16, name=f"a_raw{b}") for b in range(2)]
        b1_raw = keep.tile([P, PACK, DIM], BF16, name="b1_raw")
        b2_codes = keep.tile([P, PACK, DIM], U8, name="b2_codes")
        b2_rows = keep.tile([P, PACK], F32, name="b2_rows")
        b2_wide = keep.tile([P, PACK, DIM], BF16, name="b2_wide")
        c_sb = keep.tile([P, PACK, DIM], BF16, name="c_sb")

        def operand(name):
            return {
                "grouped": keep.tile([P, DIM, PACK], BF16, name=name + "_grouped", align_bytes=64),
                "codes": keep.tile([P, DIM], U32, name=name + "_codes", align_bytes=64),
                "scales": keep.tile([P, DIM], U8, name=name + "_scales", align_bytes=64),
            }

        xs = [operand(f"x{n}") for n in range(BATCH)]
        aa = [operand(f"a{b}") for b in range(2)]
        bb = [operand(f"b{b}") for b in range(2)]
        ts = [[operand(f"t{n}{b}") for b in range(2)] for n in range(BATCH)]

        nc.vector.memset(warm[:], 0.0)
        nc.vector.memset(zeros[:], 0.0)
        make_identity(nc, ident[:])

        row_slots = "(m t) k -> m t k"
        k_rows = "(p j) q -> p j q"

        def x_view(n):
            return x[n, :, :].rearrange(row_slots, t=PACK)

        nc.scalar.dma_start(out=b2_rows[:], in_=b2_scale.rearrange("(p j) o -> p (j o)", j=PACK))
        nc.sync.dma_start(out=b2_codes[:], in_=b2_bytes.rearrange(k_rows, j=PACK))
        nc.sync.dma_start(out=b1_raw[:], in_=b1.rearrange(k_rows, j=PACK))
        nc.sync.dma_start(out=x_raw[0][:, 0:2, :], in_=x_view(0)[:, 0:2, :])
        nc.sync.dma_start(out=x_raw[0][:, 2:4, :], in_=x_view(0)[:, 2:4, :])
        nc.sync.dma_start(out=a_raw[0][:], in_=a1.rearrange(row_slots, t=PACK))
        nc.sync.dma_start(out=a_raw[1][:], in_=a2.rearrange(row_slots, t=PACK))
        nc.sync.dma_start(out=x_raw[1][:], in_=x_view(1))
        nc.sync.dma_start(out=c_sb[:], in_=c.rearrange(row_slots, t=PACK))
        nc.sync.dma_start(out=x_raw[2][:], in_=x_view(2))
        nc.sync.dma_start(out=x_raw[3][:], in_=x_view(3))

        nc.scalar.activation(out=warm[:], in_=warm[:], func=ACT.Silu)
        def dummies(count):
            dummy = ps.tile([P, DIM], F32, name="bank")
            for i in range(count):
                nc.tensor.matmul(dummy[:], zeros[:, 0:P], zeros[:], start=True, stop=True)

        dummies(WARM)

        def copy(engine, dst, src):
            if engine == "V":
                nc.vector.tensor_copy(out=dst, in_=src)
            elif engine == "G":
                nc.gpsimd.tensor_scalar(out=dst, in0=src, scalar1=1.0, scalar2=0.0, op0=ALU.mult, op1=ALU.add)
            else:
                nc.scalar.copy(out=dst, in_=src)

        def quantise(op, first=0, width=DIM):
            cols = slice(first, first + width)
            nc.vector.quantize_mx(
                out=op["codes"][:, cols].bitcast(FP8X4),
                scales=op["scales"][:, cols],
                in_=op["grouped"][:, cols, :].rearrange("p r j -> p (r j)"),
            )

        banks = {}

        def turn(key, raw, pair):
            words = raw[:].rearrange("m t k -> m (t k)").bitcast(F32)
            bank = ps.tile([P, 2, 2, P], F32, name="bank")
            for s in range(2):
                base = 256 * (2 * pair + s)
                for u in range(2):
                    nc.tensor.transpose(bank[:, s, u, :], words[:, base + u : base + 256 : 2], ident[:])
            banks[(key, pair)] = bank

        def turn_copy(engine, key, op, pair):
            bank = banks[(key, pair)]
            words = op["grouped"][:].rearrange("p r j -> p (r j)").bitcast(F32)
            dst = words[:, 512 * pair : 512 * (pair + 1)].rearrange("p (s r u) -> p s r u", s=2, u=2)
            copy(engine, dst, bank[:].rearrange("p s u r -> p s r u"))

        def widen(engine, j):
            src = b2_codes[:, j, :].bitcast(FP8)
            if engine == "V":
                nc.vector.tensor_scalar(
                    out=b2_wide[:, j, :], in0=src, scalar1=b2_rows[:, j : j + 1], scalar2=None, op0=ALU.mult
                )
            else:
                nc.scalar.activation(out=b2_wide[:, j, :], in_=src, func=ACT.Copy, scale=b2_rows[:, j : j + 1])

        def group_b(engine, b, h):
            src = (b1_raw, b2_wide)[b]
            cols = slice(HALF * h, HALF * (h + 1))
            copy(engine, bb[b]["grouped"][:, cols, :], src[:, :, cols].rearrange("p j q -> p q j"))

        def quantise_b(b, h):
            quantise(bb[b], HALF * h, HALF)

        def mx(bank, left, rows, right, cols, start, stop):
            nc.tensor.matmul_mx(
                out=bank,
                lhsT=left["codes"][:, rows].bitcast(FP8X4),
                lhsT_scale=left["scales"][:, rows],
                rhs=right["codes"][:, cols].bitcast(FP8X4),
                rhs_scale=right["scales"][:, cols],
                start=start,
                stop=stop,
            )

        def first(n, b, q):
            bank = ps.tile([P, PACK, CHUNK], F32, name="bank")
            for t in range(PACK):
                mx(bank[:, t, :], xs[n], slice(P * t, P * (t + 1)), bb[b], slice(CHUNK * q, CHUNK * (q + 1)), True, True)
            banks[(n, b, q)] = bank

        def first_copy(engine, n, b, q):
            dst = ts[n][b]["grouped"][:, CHUNK * q : CHUNK * (q + 1), :]
            copy(engine, dst, banks[(n, b, q)][:].rearrange("p t q -> p q t"))

        def second(n, t):
            bank = ps.tile([P, DIM], F32, name="bank")
            for b in range(2):
                mx(bank[:], aa[b], slice(P * t, P * (t + 1)), ts[n][b], slice(0, DIM), b == 0, b == 1)
            banks[("z", n, t)] = bank

        def add_c(n, t):
            z = fin.tile([P, DIM], F32, name="z")
            nc.vector.tensor_tensor(out=z[:], in0=banks[("z", n, t)][:], in1=c_sb[:, t, :], op=ALU.add)
            banks[("s", n, t)] = z

        def finish(n, t):
            o = fin.tile([P, DIM], F32, name="o")
            nc.scalar.activation(out=o[:], in_=banks[("s", n, t)][:], func=ACT.Silu)
            nc.sync.dma_start(out=out[n, :, :].rearrange("(m t) q -> m t q", t=PACK)[:, t, :], in_=o[:])

        head_actions = {}
        for pair in range(2):
            head_actions[f"T:x0{pair}"] = lambda e, p=pair: turn("x0", x_raw[0], p)
            head_actions[f"C:x0{pair}"] = lambda e, p=pair: turn_copy(e, "x0", xs[0], p)
            head_actions[f"Q:x0{pair}"] = lambda e, p=pair: quantise(xs[0], HALF * p, HALF)
            for b in range(2):
                head_actions[f"T:a{b}{pair}"] = lambda e, b=b, p=pair: turn(f"a{b}", a_raw[b], p)
                head_actions[f"C:a{b}{pair}"] = lambda e, b=b, p=pair: turn_copy(e, f"a{b}", aa[b], p)
                head_actions[f"I{b}{pair}"] = lambda e, b=b, p=pair: group_b(e, b, p)
                head_actions[f"B{b}{pair}"] = lambda e, b=b, p=pair: quantise_b(b, p)
        for pair in range(2):
            head_actions[f"T1.{pair}"] = lambda e, p=pair: turn("x1", x_raw[1], p)
            head_actions[f"C1.{pair}"] = lambda e, p=pair: turn_copy(e, "x1", xs[1], p)
        for b in range(2):
            head_actions[f"Q:a{b}"] = lambda e, b=b: quantise(aa[b])
        for j in range(PACK):
            head_actions[f"W{j}"] = lambda e, j=j: widen(e, j)
            head_actions[f"D{j}"] = lambda e, j=j: dummies(2)

        for key, engine in HEAD:
            head_actions[key](engine)

        def whole_second(n, t):
            second(n, t)
            add_c(n, t)

        for n in range(BATCH):
            for k in range(8):
                b, q = k // 4, k % 4
                if n >= 2 and k == N0POS:
                    second(n - 2, 0)
                first(n, b, q)
                first_copy("V" if k in ON_VECTOR[n] else "S", n, b, q)
                if n + 1 < BATCH and k == QPOS:
                    quantise(xs[n + 1])
            if n >= 2:
                second(n - 2, 1)
                add_c(n - 2, 0)
            quantise(ts[n][0])
            if n + 2 < BATCH:
                turn(f"x{n + 2}", x_raw[n + 2], 0)
                turn(f"x{n + 2}", x_raw[n + 2], 1)
                turn_copy("V", f"x{n + 2}", xs[n + 2], 0)
                turn_copy("S", f"x{n + 2}", xs[n + 2], 1)
            if n >= 2:
                add_c(n - 2, 1)
            quantise(ts[n][1])
            for job in FINISH_EARLY[n]:
                finish(*job)
        tail = [(n, t) for n in range(BATCH) for t in range(PACK) if n >= 2 or t >= 2]
        for job in FINISH_EARLY[4]:
            finish(*job)
        for n, t in tail:
            whole_second(n, t)
            finish(n, t)
